import numpy as np
import ml_dtypes


def mxq(x, axis, fmt="e4m3"):
    dtype, down = {"e4m3": (ml_dtypes.float8_e4m3fn, 7), "e5m2": (ml_dtypes.float8_e5m2, 14)}[fmt]
    v = np.moveaxis(np.asarray(x, np.float32).astype(ml_dtypes.bfloat16).astype(np.float64), axis, -1)
    blocks = v.reshape(v.shape[:-1] + (-1, 32))
    amax = np.abs(blocks).max(-1, keepdims=True)
    byte = np.maximum(np.where(amax > 0, np.frexp(amax)[1] - 1 + 127, 0) - down, 1)
    scale = np.exp2(byte - 127.0)
    codes = (blocks / scale).astype(np.float32).astype(dtype).astype(np.float64)
    return np.moveaxis((codes * scale).reshape(v.shape), -1, axis)


WIDE = False


def mx_kscale(k):
    if not WIDE:
        return np.ones(k)
    levels = np.array([10, -10, 5, -5, 0])
    if k % 512:
        return np.exp2(np.random.permutation(np.resize(levels, k // 32))).repeat(32)
    a = np.empty((k // 512, 16))
    for p in range(k // 512):
        a[p, :8] = np.random.permutation(np.resize(levels, 8))
        for g in range(8):
            far = levels[np.abs(levels - a[p, g]) >= 10]
            a[p, g + 8] = far[np.random.randint(len(far))]
    return np.exp2(a.ravel()).repeat(32)


def f64(x):
    return np.asarray(x).astype(np.float64)


def striped(idx):
    return np.tile(idx.reshape(-1, 16).T, (8, 1)).astype(np.uint16)


def unstriped(offs):
    return offs[:16].T.reshape(-1).astype(np.int64)


def sigmoid(v):
    return 1.0 / (1.0 + np.exp(-np.maximum(v, -700.0)))


K, T, E, C, H, N = 1024, 512, 4, 128, 1024, 128


def by_expert(wq, xq):
    return np.concatenate([wq[e].T @ xq[:, e * C:(e + 1) * C] for e in range(E)], axis=1)


def setup_inputs():
    n = np.random.standard_normal
    s = mx_kscale(K)[:, None]
    u = mx_kscale(H)
    return {
        "xT": (n((K, T)) * s).astype(np.float32),
        "w1": (n((E, K, H)) / np.sqrt(K) / s[None]).astype(np.float32),
        "w3": (n((E, K, H)) / np.sqrt(K) / s[None] * u[None, None, :]).astype(np.float32),
        "w2": (n((E, H, N)) / np.sqrt(H) / u[None, :, None]).astype(np.float32),
        "gate": np.tile(np.random.uniform(0.2, 1.0, E * C), (N, 1)).astype(np.float32),
        "offs": striped(np.random.permutation(T)[:E * C]),
    }


def reference(xT, w1, w3, w2, gate, offs):
    idx = unstriped(offs)
    xq = mxq(f64(xT)[:, idx], 0, "e4m3")
    h = sigmoid(by_expert(mxq(f64(w1), 1, "e4m3"), xq))
    h = h * by_expert(mxq(f64(w3), 1, "e4m3"), xq)
    y = by_expert(mxq(f64(w2), 1, "e4m3"), mxq(h, 0, "e4m3"))
    out = np.zeros((N, T))
    out[:, idx] = f64(gate) * y
    return out

@@ -1,0 +1,211 @@
+from contextlib import ExitStack
+
+import concourse.mybir as mybir
+
+K, T, E, C, H, N = 1024, 512, 4, 128, 1024, 128
+FLOPS = 2 * E * C * (2 * K * H + H * N)
+
+F32 = mybir.dt.float32
+BF16 = mybir.dt.bfloat16
+U32 = mybir.dt.uint32
+U16 = mybir.dt.uint16
+U8 = mybir.dt.uint8
+FP8X4 = mybir.dt.float8_e4m3fn_x4
+MULT = mybir.AluOpType.mult
+SIGMOID = mybir.ActivationFunctionType.Sigmoid
+
+P = 128
+J = 4
+PASS = P * J
+G = K // PASS
+B = H // PASS
+
+
+def tile_routed_moe_kernel(tc, xT, w1, w3, w2, gate, offs, out):
+    nc = tc.nc
+
+    with ExitStack() as ctx:
+        keep = ctx.enter_context(tc.tile_pool(name="keep", bufs=1))
+        raws = ctx.enter_context(tc.tile_pool(name="raws", bufs=6))
+        groups = ctx.enter_context(tc.tile_pool(name="groups", bufs=3))
+        weights = ctx.enter_context(tc.tile_pool(name="weights", bufs=3))
+        work = ctx.enter_context(tc.tile_pool(name="work", bufs=3))
+        psum = ctx.enter_context(tc.psum_pool(name="psum", bufs=2))
+
+        offsets = keep.tile([P, E * C // 16], U16, name="offsets")
+        gates = keep.tile([P, E * C], F32, name="gates")
+        window = keep.tile([P, T], F32, name="window")
+        slot_codes = keep.tile([P, G, E * C], U32, name="slot_codes", align_bytes=64)
+        slot_scales = keep.tile([P, G, E * C], U8, name="slot_scales", align_bytes=64)
+
+        def copy_on(engine, dst, src):
+            if engine == 0:
+                nc.vector.tensor_copy(dst, src)
+            else:
+                nc.scalar.copy(dst, src)
+
+        token_codes, token_scales, token_raw = [], [], []
+        for g in range(G):
+            codes = keep.tile([P, T], U32, name=f"token_codes{g}", align_bytes=64)
+            scales = keep.tile([P, T], U8, name=f"token_scales{g}", align_bytes=64)
+            nc.gpsimd.memset(scales[:], 0)
+            token_codes.append(codes)
+            token_scales.append(scales)
+            raw = raws.tile([P, J * T], F32, name="raw")
+            nc.sync.dma_start(out=raw[:], in_=xT.rearrange("(g p j) n -> g p (j n)", p=P, j=J)[g])
+            token_raw.append(raw[:].rearrange("p (j n) -> p j n", j=J))
+            if g == 0:
+                nc.sync.dma_start(offsets[:], offs)
+        for g in range(G):
+            grouped = keep.tile([P, T, J], BF16, name=f"token_grouped{g}", align_bytes=64)
+            copy_on(g, grouped[:].rearrange("p (c i) j -> p c j i", i=4),
+                    token_raw[g].rearrange("p j (c i) -> p c j i", i=4))
+            nc.vector.quantize_mx(out=token_codes[g][:].bitcast(FP8X4), scales=token_scales[g][:],
+                                  in_=grouped[:].rearrange("p n j -> p (n j)"))
+        piece = 256
+        for s in range(E * C // piece):
+            cols = offsets[:, s * (piece // 16):(s + 1) * (piece // 16)]
+            for g in range(G):
+                nc.vector.tensor_copy(slot_codes[:, g, s * piece:(s + 1) * piece], token_codes[g][:].indirect(cols))
+                nc.vector.tensor_copy(slot_scales[:, g, s * piece:(s + 1) * piece], token_scales[g][:].indirect(cols))
+
+        def load_pass(dram, g):
+            raw = raws.tile([P, J * H], F32, name="raw")
+            nc.sync.dma_start(out=raw[:], in_=dram.rearrange("(g p j) c -> g p (j c)", p=P, j=J)[g])
+            return raw[:].rearrange("p (j c) -> p j c", j=J)
+
+        def interleave(engine, grouped, raw, c0, m0, m1):
+            copy_on(engine, grouped[:].rearrange("p (t m j) -> p m j t", t=J, j=J)[:, m0:m1],
+                    raw[:, :, c0 + J * m0:c0 + J * m1].rearrange("p j (m t) -> p m j t", t=J))
+
+        def quantize(grouped, codes, scales, c0, parts):
+            width = PASS // parts
+            for i in range(parts):
+                cols = slice(c0 + i * width, c0 + (i + 1) * width)
+                nc.vector.quantize_mx(out=codes[:, cols].bitcast(FP8X4), scales=scales[:, cols],
+                                      in_=grouped[:, i * width * J:(i + 1) * width * J])
+
+        def new_operand(name):
+            codes = weights.tile([P, G, H], U32, name=f"{name}_codes", align_bytes=64)
+            scales = weights.tile([P, G, H], U8, name=f"{name}_scales", align_bytes=64)
+            return codes, scales
+
+        def block(raw, c0, b, cut):
+            grouped = groups.tile([P, PASS * J], BF16, name=f"grouped{b}", align_bytes=64)
+            if cut > 0:
+                interleave(0, grouped, raw, c0, 0, cut)
+            if cut < P:
+                interleave(1, grouped, raw, c0, cut, P)
+            return grouped
+
+        def quantize_pass(grouped, operand, g, b, parts):
+            quantize(grouped, operand[0][:, g], operand[1][:, g], b * PASS, parts)
+
+        def whole_pass(dram, operand, g, cuts):
+            raw = load_pass(dram, g)
+            blocks = [block(raw, b * PASS, b, cuts[b]) for b in range(B)]
+            for b in range(B):
+                quantize_pass(blocks[b], operand, g, b, 1)
+
+        def load_w2(e):
+            raw = raws.tile([P, B, J * N], F32, name="raw")
+            nc.sync.dma_start(out=raw[:], in_=w2[e].rearrange("(b p j) n -> p b (j n)", p=P, j=J))
+            return raw[:].rearrange("p b (j n) -> p b j n", j=J)
+
+        def interleave_w2(raw, b, engine):
+            grouped = groups.tile([P, N, J], BF16, name=f"w2_grouped{b}", align_bytes=64)
+            copy_on(engine, grouped[:].rearrange("p (c i) j -> p c j i", i=4),
+                    raw[:, b].rearrange("p j (c i) -> p c j i", i=4))
+            return grouped
+
+        def new_w2():
+            codes = weights.tile([P, B, N], U32, name="w2_codes", align_bytes=64)
+            scales = weights.tile([P, B, N], U8, name="w2_scales", align_bytes=64)
+            return codes, scales
+
+        def quantize_w2(grouped, operand, b):
+            nc.vector.quantize_mx(out=operand[0][:, b].bitcast(FP8X4), scales=operand[1][:, b],
+                                  in_=grouped[:].rearrange("p n j -> p (n j)"))
+
+        def prepare_w2(e):
+            raw, operand = load_w2(e), new_w2()
+            blocks = [interleave_w2(raw, b, b) for b in range(B)]
+            for b in range(B):
+                quantize_w2(blocks[b], operand, b)
+            return operand
+
+        def hidden_sums(operand, e, b, name):
+            codes, scales = operand
+            acc = psum.tile([P, J, C], F32, name=name)
+            slots = slice(e * C, (e + 1) * C)
+            for t in range(J):
+                cols = slice(b * PASS + t * P, b * PASS + (t + 1) * P)
+                for g in range(G):
+                    nc.tensor.matmul_mx(
+                        out=acc[:, t, :],
+                        lhsT=codes[:, g, cols].bitcast(FP8X4), lhsT_scale=scales[:, g, cols],
+                        rhs=slot_codes[:, g, slots].bitcast(FP8X4), rhs_scale=slot_scales[:, g, slots],
+                        start=(g == 0), stop=(g == G - 1))
+            return acc
+
+        def open_gates(operand, e, b):
+            a = hidden_sums(operand, e, b, "a")
+            sig = work.tile([P, J, C], F32, name=f"sig{b}")
+            nc.scalar.activation(sig[:], a[:], SIGMOID)
+            return sig
+
+        def product(v, sig):
+            h = work.tile([P, C, J], BF16, name="h", align_bytes=64)
+            nc.vector.tensor_tensor(h[:], v[:].rearrange("p t n -> p n t"), sig[:].rearrange("p t n -> p n t"), MULT)
+            return h
+
+        def quantize_hidden(h, h_operand, b):
+            nc.vector.quantize_mx(out=h_operand[0][:, b, :].bitcast(FP8X4), scales=h_operand[1][:, b, :],
+                                  in_=h[:].rearrange("p n t -> p (n t)"))
+
+        def second_sums(w2_operand, h_operand):
+            y = psum.tile([N, C], F32, name="y")
+            for b in range(B):
+                nc.tensor.matmul_mx(
+                    out=y[:],
+                    lhsT=w2_operand[0][:, b, :].bitcast(FP8X4), lhsT_scale=w2_operand[1][:, b, :],
+                    rhs=h_operand[0][:, b, :].bitcast(FP8X4), rhs_scale=h_operand[1][:, b, :],
+                    start=(b == 0), stop=(b == B - 1))
+            y_sb = work.tile([N, C], F32, name="y_sb")
+            nc.scalar.copy(y_sb[:], y[:])
+            return y_sb
+
+        def scatter(e, y_sb):
+            nc.vector.tensor_tensor(window[:].indirect(offsets[:, e * (C // 16):(e + 1) * (C // 16)]),
+                                    y_sb[:], gates[:, e * C:(e + 1) * C], MULT)
+
+        def new_hidden(e):
+            codes = keep.tile([P, B, C], U32, name=f"h_codes{e}", align_bytes=64)
+            scales = keep.tile([P, B, C], U8, name=f"h_scales{e}", align_bytes=64)
+            return codes, scales
+
+        def prepare_late(e, engines):
+            raw, operand = load_w2(e), new_w2()
+            for b in range(B):
+                quantize_w2(interleave_w2(raw, b, engines[b]), operand, b)
+            return operand
+
+        late = []
+        for e in range(E):
+            op1, op3, h_op = new_operand("w1"), new_operand("w3"), new_hidden(e)
+            for g in range(G):
+                whole_pass(w1[e], op1, g, (P, 0))
+            sigs = [open_gates(op1, e, b) for b in range(B)]
+            for g in range(G):
+                whole_pass(w3[e], op3, g, (80, 88) if (e, g) == (E - 1, G - 1) else (P, 0))
+            if e == 0:
+                nc.sync.dma_start(gates[:], gate)
+            for b in range(B):
+                quantize_hidden(product(hidden_sums(op3, e, b, "v"), sigs[b]), h_op, b)
+            if e < 2:
+                scatter(e, second_sums(prepare_w2(e), h_op))
+            else:
+                late.append((e, h_op))
+        for e, h_op in late:
+            scatter(e, second_sums(prepare_late(e, (1, 1)), h_op))
+        nc.sync.dma_start(out, window[:])

@@ -154,16 +154,20 @@ def tile_routed_moe_kernel(tc, xT, w1, w3, w2, gate, offs, out):
             nc.scalar.activation(sig[:], a[:], SIGMOID)
             return sig
 
-        def product(v, sig):
-            h = work.tile([P, C, J], BF16, name="h", align_bytes=64)
-            nc.vector.tensor_tensor(h[:], v[:].rearrange("p t n -> p n t"), sig[:].rearrange("p t n -> p n t"), MULT)
+        def product_into(h, v, sig):
+            nc.vector.tensor_tensor(h.rearrange("p (n t) -> p n t", t=J), v[:].rearrange("p t n -> p n t"),
+                                    sig[:].rearrange("p t n -> p n t"), MULT)
             return h
+
+        def product(v, sig):
+            h = work.tile([P, C * J], BF16, name="h", align_bytes=64)
+            return product_into(h[:], v, sig)
 
         def quantize_hidden(h, h_operand, b):
             nc.vector.quantize_mx(out=h_operand[0][:, b, :].bitcast(FP8X4), scales=h_operand[1][:, b, :],
-                                  in_=h[:].rearrange("p n t -> p (n t)"))
+                                  in_=h)
 
-        def second_sums(w2_operand, h_operand):
+        def second_sums(w2_operand, h_operand, y_sb):
             y = psum.tile([N, C], F32, name="y")
             for b in range(B):
                 nc.tensor.matmul_mx(
@@ -171,41 +175,79 @@ def tile_routed_moe_kernel(tc, xT, w1, w3, w2, gate, offs, out):
                     lhsT=w2_operand[0][:, b, :].bitcast(FP8X4), lhsT_scale=w2_operand[1][:, b, :],
                     rhs=h_operand[0][:, b, :].bitcast(FP8X4), rhs_scale=h_operand[1][:, b, :],
                     start=(b == 0), stop=(b == B - 1))
-            y_sb = work.tile([N, C], F32, name="y_sb")
-            nc.scalar.copy(y_sb[:], y[:])
+            nc.scalar.copy(y_sb, y[:])
             return y_sb
+
+        def new_y():
+            y_sb = work.tile([N, C], F32, name="y_sb")
+            return y_sb[:]
 
         def scatter(e, y_sb):
             nc.vector.tensor_tensor(window[:].indirect(offsets[:, e * (C // 16):(e + 1) * (C // 16)]),
-                                    y_sb[:], gates[:, e * C:(e + 1) * C], MULT)
+                                    y_sb, gates[:, e * C:(e + 1) * C], MULT)
 
         def new_hidden(e):
             codes = keep.tile([P, B, C], U32, name=f"h_codes{e}", align_bytes=64)
             scales = keep.tile([P, B, C], U8, name=f"h_scales{e}", align_bytes=64)
             return codes, scales
 
-        def prepare_late(e, engines):
-            raw, operand = load_w2(e), new_w2()
-            for b in range(B):
-                quantize_w2(interleave_w2(raw, b, engines[b]), operand, b)
-            return operand
+        def interleave_whole_w2(raw, engine):
+            grouped = groups.tile([P, B, N, J], BF16, name="w2_both", align_bytes=64, bufs=2)
+            copy_on(engine, grouped[:].rearrange("p b (c i) j -> p b c j i", i=4),
+                    raw.rearrange("p b j (c i) -> p b c j i", i=4))
+            return grouped
 
-        late = []
+        def quantize_both(values, operand):
+            nc.vector.quantize_mx(out=operand[0][:].rearrange("p b n -> p (b n)").bitcast(FP8X4),
+                                  scales=operand[1][:].rearrange("p b n -> p (b n)"), in_=values)
+
+        def load_half(dram, g, b):
+            raw = raws.tile([P, J, PASS], F32, name="raw")
+            rows = dram.rearrange("(g p j) c -> g p j c", p=P, j=J)[g]
+            nc.sync.dma_start(out=raw[:], in_=rows[:, :, b * PASS:(b + 1) * PASS])
+            return raw[:]
+
+        h_ops = []
         for e in range(E):
             op1, op3, h_op = new_operand("w1"), new_operand("w3"), new_hidden(e)
-            for g in range(G):
-                whole_pass(w1[e], op1, g, (P, 0))
-            sigs = [open_gates(op1, e, b) for b in range(B)]
-            for g in range(G):
-                whole_pass(w3[e], op3, g, (80, 88) if (e, g) == (E - 1, G - 1) else (P, 0))
-            if e == 0:
-                nc.sync.dma_start(gates[:], gate)
-            for b in range(B):
-                quantize_hidden(product(hidden_sums(op3, e, b, "v"), sigs[b]), h_op, b)
-            if e < 2:
-                scatter(e, second_sums(prepare_w2(e), h_op))
-            else:
-                late.append((e, h_op))
-        for e, h_op in late:
-            scatter(e, second_sums(prepare_late(e, (1, 1)), h_op))
+            h_ops.append(h_op)
+            if e < E - 1:
+                for g in range(G):
+                    whole_pass(w1[e], op1, g, (P, 0))
+                sigs = [open_gates(op1, e, b) for b in range(B)]
+                for g in range(G):
+                    whole_pass(w3[e], op3, g, (P, 0))
+                if e == 0:
+                    nc.sync.dma_start(gates[:], gate)
+                for b in range(B):
+                    quantize_hidden(product(hidden_sums(op3, e, b, "v"), sigs[b]), h_op, b)
+                if e < E - 2:
+                    scatter(e, second_sums(prepare_w2(e), h_op, new_y()))
+        whole_pass(w1[e], op1, 0, (P, 0))
+        whole_pass(w1[e], op1, 1, (88, 56))
+        sigs = [open_gates(op1, e, 0)]
+        whole_pass(w3[e], op3, 0, (88, 48))
+        sigs.append(open_gates(op1, e, 1))
+        raw_a = load_half(w3[e], 1, 0)
+        raw_b = load_half(w3[e], 1, 1)
+        raw_c, op_c = load_w2(e - 1), new_w2()
+        raw_d, op_d = load_w2(e), new_w2()
+        quantize_pass(block(raw_a, 0, 0, 56), op3, 1, 0, 1)
+        v0 = hidden_sums(op3, e, 0, "v")
+        grouped_b = block(raw_b, 0, 1, 84)
+        quantize_pass(grouped_b, op3, 1, 1, 4)
+        v1 = hidden_sums(op3, e, 1, "v")
+        both_c = interleave_whole_w2(raw_c, 1)
+        both_d = interleave_whole_w2(raw_d, 1)
+        h0 = product_into(grouped_b[:, PASS:2 * PASS], v0, sigs[0])
+        values_c = both_c[:].rearrange("p b n j -> p (b n j)")
+        quantize_both(values_c, op_c)
+        y_c = second_sums(op_c, h_ops[e - 1], raw_d[:, 0, 0])
+        h1 = product_into(values_c[:, 0:PASS], v1, sigs[1])
+        quantize_hidden(h0, h_op, 0)
+        quantize_both(both_d[:].rearrange("p b n j -> p (b n j)"), op_d)
+        quantize_hidden(h1, h_op, 1)
+        y_d = second_sums(op_d, h_op, new_y())
+        scatter(e - 1, y_c)
+        scatter(e, y_d)
         nc.sync.dma_start(out, window[:])

@@ -32,8 +32,10 @@ def tile_routed_moe_kernel(tc, xT, w1, w3, w2, gate, offs, out):
         work = ctx.enter_context(tc.tile_pool(name="work", bufs=3))
         psum = ctx.enter_context(tc.psum_pool(name="psum", bufs=2))
 
+        pairs = ctx.enter_context(tc.psum_pool(name="pairs", bufs=1))
+
         offsets = keep.tile([P, E * C // 16], U16, name="offsets")
-        gates = keep.tile([P, E * C], F32, name="gates")
+        gates = keep.tile([P, 2 * C], F32, name="gates")
         window = keep.tile([P, T], F32, name="window")
         slot_codes = keep.tile([P, G, E * C], U32, name="slot_codes", align_bytes=64)
         slot_scales = keep.tile([P, G, E * C], U8, name="slot_scales", align_bytes=64)
@@ -51,7 +53,7 @@ def tile_routed_moe_kernel(tc, xT, w1, w3, w2, gate, offs, out):
             nc.gpsimd.memset(scales[:], 0)
             token_codes.append(codes)
             token_scales.append(scales)
-            raw = raws.tile([P, J * T], F32, name="raw")
+            raw = raws.tile([P, J * T], F32, name="raw", align_bytes=64)
             nc.sync.dma_start(out=raw[:], in_=xT.rearrange("(g p j) n -> g p (j n)", p=P, j=J)[g])
             token_raw.append(raw[:].rearrange("p (j n) -> p j n", j=J))
             if g == 0:
@@ -70,7 +72,7 @@ def tile_routed_moe_kernel(tc, xT, w1, w3, w2, gate, offs, out):
                 nc.vector.tensor_copy(slot_scales[:, g, s * piece:(s + 1) * piece], token_scales[g][:].indirect(cols))
 
         def load_pass(dram, g):
-            raw = raws.tile([P, J * H], F32, name="raw")
+            raw = raws.tile([P, J * H], F32, name="raw", align_bytes=64)
             nc.sync.dma_start(out=raw[:], in_=dram.rearrange("(g p j) c -> g p (j c)", p=P, j=J)[g])
             return raw[:].rearrange("p (j c) -> p j c", j=J)
 
@@ -108,7 +110,7 @@ def tile_routed_moe_kernel(tc, xT, w1, w3, w2, gate, offs, out):
                 quantize_pass(blocks[b], operand, g, b, 1)
 
         def load_w2(e):
-            raw = raws.tile([P, B, J * N], F32, name="raw")
+            raw = raws.tile([P, B, J * N], F32, name="raw", align_bytes=64)
             nc.sync.dma_start(out=raw[:], in_=w2[e].rearrange("(b p j) n -> p b (j n)", p=P, j=J))
             return raw[:].rearrange("p b (j n) -> p b j n", j=J)
 
@@ -148,6 +150,27 @@ def tile_routed_moe_kernel(tc, xT, w1, w3, w2, gate, offs, out):
                         start=(g == 0), stop=(g == G - 1))
             return acc
 
+        def paired_sums(operand, e, b):
+            codes, scales = operand
+            slots = slice(e * C, (e + 1) * C)
+            banks = [pairs.tile([P, 2, C], F32, name=f"pair{u}") for u in range(2)]
+            for t in range(J):
+                cols = slice(b * PASS + t * P, b * PASS + (t + 1) * P)
+                for g in range(G):
+                    nc.tensor.matmul_mx(
+                        out=banks[t // 2][:, t % 2, :],
+                        lhsT=codes[:, g, cols].bitcast(FP8X4), lhsT_scale=scales[:, g, cols],
+                        rhs=slot_codes[:, g, slots].bitcast(FP8X4), rhs_scale=slot_scales[:, g, slots],
+                        start=(g == 0), stop=(g == G - 1))
+            return banks
+
+        def paired_product(h, banks, sig):
+            for u in range(2):
+                nc.vector.tensor_tensor(h.rearrange("p (n t) -> p n t", t=J)[:, :, 2 * u:2 * u + 2],
+                                        banks[u][:].rearrange("p t n -> p n t"),
+                                        sig[:, 2 * u:2 * u + 2].rearrange("p t n -> p n t"), MULT)
+            return h
+
         def open_gates(operand, e, b):
             a = hidden_sums(operand, e, b, "a")
             sig = work.tile([P, J, C], F32, name=f"sig{b}")
@@ -182,9 +205,9 @@ def tile_routed_moe_kernel(tc, xT, w1, w3, w2, gate, offs, out):
             y_sb = work.tile([N, C], F32, name="y_sb")
             return y_sb[:]
 
-        def scatter(e, y_sb):
+        def scatter(e, y_sb, weight):
             nc.vector.tensor_tensor(window[:].indirect(offsets[:, e * (C // 16):(e + 1) * (C // 16)]),
-                                    y_sb, gates[:, e * C:(e + 1) * C], MULT)
+                                    y_sb, weight, MULT)
 
         def new_hidden(e):
             codes = keep.tile([P, B, C], U32, name=f"h_codes{e}", align_bytes=64)
@@ -201,10 +224,10 @@ def tile_routed_moe_kernel(tc, xT, w1, w3, w2, gate, offs, out):
             nc.vector.quantize_mx(out=operand[0][:].rearrange("p b n -> p (b n)").bitcast(FP8X4),
                                   scales=operand[1][:].rearrange("p b n -> p (b n)"), in_=values)
 
-        def load_half(dram, g, b):
-            raw = raws.tile([P, J, PASS], F32, name="raw")
+        def load_columns(dram, g, c0, c1):
+            raw = raws.tile([P, J, c1 - c0], F32, name="raw", align_bytes=64)
             rows = dram.rearrange("(g p j) c -> g p j c", p=P, j=J)[g]
-            nc.sync.dma_start(out=raw[:], in_=rows[:, :, b * PASS:(b + 1) * PASS])
+            nc.sync.dma_start(out=raw[:], in_=rows[:, :, c0:c1])
             return raw[:]
 
         h_ops = []
@@ -218,36 +241,45 @@ def tile_routed_moe_kernel(tc, xT, w1, w3, w2, gate, offs, out):
                 for g in range(G):
                     whole_pass(w3[e], op3, g, (P, 0))
                 if e == 0:
-                    nc.sync.dma_start(gates[:], gate)
+                    nc.sync.dma_start(gates[:], gate[:, :2 * C])
                 for b in range(B):
                     quantize_hidden(product(hidden_sums(op3, e, b, "v"), sigs[b]), h_op, b)
                 if e < E - 2:
-                    scatter(e, second_sums(prepare_w2(e), h_op, new_y()))
+                    scatter(e, second_sums(prepare_w2(e), h_op, new_y()), gates[:, e * C:(e + 1) * C])
         whole_pass(w1[e], op1, 0, (P, 0))
         whole_pass(w1[e], op1, 1, (88, 56))
         sigs = [open_gates(op1, e, 0)]
-        whole_pass(w3[e], op3, 0, (88, 48))
-        sigs.append(open_gates(op1, e, 1))
-        raw_a = load_half(w3[e], 1, 0)
-        raw_b = load_half(w3[e], 1, 1)
+        raw_1 = load_columns(w3[e], 0, 0, PASS)
+        raw_2 = load_columns(w3[e], 1, 0, PASS)
+        raw_3 = load_columns(w3[e], 0, PASS, H)
+        raw_4 = load_columns(w3[e], 1, PASS, PASS + J * 64)
+        raw_5 = load_columns(w3[e], 1, PASS + J * 64, H)
         raw_c, op_c = load_w2(e - 1), new_w2()
         raw_d, op_d = load_w2(e), new_w2()
-        quantize_pass(block(raw_a, 0, 0, 56), op3, 1, 0, 1)
+        late_gates = raws.tile([P, 2 * C], F32, name="raw", align_bytes=64)
+        nc.sync.dma_start(late_gates[:], gate[:, 2 * C:])
+        quantize_pass(block(raw_1, 0, 0, 64), op3, 0, 0, 1)
+        quantize_pass(block(raw_2, 0, 0, 64), op3, 1, 0, 1)
+        sigs.append(open_gates(op1, e, 1))
         v0 = hidden_sums(op3, e, 0, "v")
-        grouped_b = block(raw_b, 0, 1, 84)
+        quantize_pass(block(raw_3, 0, 1, 64), op3, 0, 1, 1)
+        h0 = product(v0, sigs[0])
+        grouped_b = groups.tile([P, PASS * J], BF16, name="grouped1", align_bytes=64)
+        interleave(1, grouped_b, raw_4, 0, 0, 64)
+        interleave(0, grouped_b, raw_5, -J * 64, 64, 104)
+        interleave(1, grouped_b, raw_5, -J * 64, 104, P)
         quantize_pass(grouped_b, op3, 1, 1, 4)
-        v1 = hidden_sums(op3, e, 1, "v")
+        v1 = paired_sums(op3, e, 1)
         both_c = interleave_whole_w2(raw_c, 1)
         both_d = interleave_whole_w2(raw_d, 1)
-        h0 = product_into(grouped_b[:, PASS:2 * PASS], v0, sigs[0])
         values_c = both_c[:].rearrange("p b n j -> p (b n j)")
         quantize_both(values_c, op_c)
         y_c = second_sums(op_c, h_ops[e - 1], raw_d[:, 0, 0])
-        h1 = product_into(values_c[:, 0:PASS], v1, sigs[1])
+        h1 = paired_product(raw_c.rearrange("p b j n -> p (b j n)")[:, 0:PASS // 2].bitcast(BF16), v1, sigs[1])
         quantize_hidden(h0, h_op, 0)
         quantize_both(both_d[:].rearrange("p b n j -> p (b n j)"), op_d)
         quantize_hidden(h1, h_op, 1)
         y_d = second_sums(op_d, h_op, new_y())
-        scatter(e - 1, y_c)
-        scatter(e, y_d)
+        scatter(e - 1, y_c, late_gates[:, :C])
+        scatter(e, y_d, late_gates[:, C:])
         nc.sync.dma_start(out, window[:])

@@ -77,8 +77,8 @@ def tile_routed_moe_kernel(tc, xT, w1, w3, w2, gate, offs, out):
             return raw[:].rearrange("p (j c) -> p j c", j=J)
 
         def interleave(engine, grouped, raw, c0, m0, m1):
-            copy_on(engine, grouped[:].rearrange("p (t m j) -> p m j t", t=J, j=J)[:, m0:m1],
-                    raw[:, :, c0 + J * m0:c0 + J * m1].rearrange("p j (m t) -> p m j t", t=J))
+            copy_on(engine, grouped[:].rearrange("p (u v m j) -> p u m j v", u=2, v=2, j=J)[:, :, m0:m1],
+                    raw[:, :, c0 + J * m0:c0 + J * m1].rearrange("p j (m u v) -> p u m j v", u=2, v=2))
 
         def quantize(grouped, codes, scales, c0, parts):
             width = PASS // parts

@@ -35,8 +35,8 @@ def tile_routed_moe_kernel(tc, xT, w1, w3, w2, gate, offs, out):
         pairs = ctx.enter_context(tc.psum_pool(name="pairs", bufs=1))
 
         offsets = keep.tile([P, E * C // 16], U16, name="offsets")
-        gates = keep.tile([P, 2 * C], F32, name="gates")
-        window = keep.tile([P, T], F32, name="window")
+        gates = keep.tile([P, 2 * C], F32, name="gates", align_bytes=512)
+        window = keep.tile([P, T], F32, name="window", align_bytes=512)
         slot_codes = keep.tile([P, G, E * C], U32, name="slot_codes", align_bytes=64)
         slot_scales = keep.tile([P, G, E * C], U8, name="slot_scales", align_bytes=64)
 
@@ -53,7 +53,7 @@ def tile_routed_moe_kernel(tc, xT, w1, w3, w2, gate, offs, out):
             nc.gpsimd.memset(scales[:], 0)
             token_codes.append(codes)
             token_scales.append(scales)
-            raw = raws.tile([P, J * T], F32, name="raw", align_bytes=64)
+            raw = raws.tile([P, J * T], F32, name="raw", align_bytes=512)
             nc.sync.dma_start(out=raw[:], in_=xT.rearrange("(g p j) n -> g p (j n)", p=P, j=J)[g])
             token_raw.append(raw[:].rearrange("p (j n) -> p j n", j=J))
             if g == 0:
@@ -72,7 +72,7 @@ def tile_routed_moe_kernel(tc, xT, w1, w3, w2, gate, offs, out):
                 nc.vector.tensor_copy(slot_scales[:, g, s * piece:(s + 1) * piece], token_scales[g][:].indirect(cols))
 
         def load_pass(dram, g):
-            raw = raws.tile([P, J * H], F32, name="raw", align_bytes=64)
+            raw = raws.tile([P, J * H], F32, name="raw", align_bytes=512)
             nc.sync.dma_start(out=raw[:], in_=dram.rearrange("(g p j) c -> g p (j c)", p=P, j=J)[g])
             return raw[:].rearrange("p (j c) -> p j c", j=J)
 
@@ -110,7 +110,7 @@ def tile_routed_moe_kernel(tc, xT, w1, w3, w2, gate, offs, out):
                 quantize_pass(blocks[b], operand, g, b, 1)
 
         def load_w2(e):
-            raw = raws.tile([P, B, J * N], F32, name="raw", align_bytes=64)
+            raw = raws.tile([P, B, J * N], F32, name="raw", align_bytes=512)
             nc.sync.dma_start(out=raw[:], in_=w2[e].rearrange("(b p j) n -> p b (j n)", p=P, j=J))
             return raw[:].rearrange("p b (j n) -> p b j n", j=J)
 
@@ -225,7 +225,7 @@ def tile_routed_moe_kernel(tc, xT, w1, w3, w2, gate, offs, out):
                                   scales=operand[1][:].rearrange("p b n -> p (b n)"), in_=values)
 
         def load_columns(dram, g, c0, c1):
-            raw = raws.tile([P, J, c1 - c0], F32, name="raw", align_bytes=64)
+            raw = raws.tile([P, J, c1 - c0], F32, name="raw", align_bytes=512)
             rows = dram.rearrange("(g p j) c -> g p j c", p=P, j=J)[g]
             nc.sync.dma_start(out=raw[:], in_=rows[:, :, c0:c1])
             return raw[:]
@@ -256,7 +256,7 @@ def tile_routed_moe_kernel(tc, xT, w1, w3, w2, gate, offs, out):
         raw_5 = load_columns(w3[e], 1, PASS + J * 64, H)
         raw_c, op_c = load_w2(e - 1), new_w2()
         raw_d, op_d = load_w2(e), new_w2()
-        late_gates = raws.tile([P, 2 * C], F32, name="raw", align_bytes=64)
+        late_gates = raws.tile([P, 2 * C], F32, name="raw", align_bytes=512)
         nc.sync.dma_start(late_gates[:], gate[:, 2 * C:])
         quantize_pass(block(raw_1, 0, 0, 64), op3, 0, 0, 1)
         quantize_pass(block(raw_2, 0, 0, 64), op3, 1, 0, 1)

@@ -28,7 +28,7 @@ def tile_routed_moe_kernel(tc, xT, w1, w3, w2, gate, offs, out):
         keep = ctx.enter_context(tc.tile_pool(name="keep", bufs=1))
         raws = ctx.enter_context(tc.tile_pool(name="raws", bufs=6))
         groups = ctx.enter_context(tc.tile_pool(name="groups", bufs=3))
-        weights = ctx.enter_context(tc.tile_pool(name="weights", bufs=3))
+        weights = ctx.enter_context(tc.tile_pool(name="weights", bufs=2))
         work = ctx.enter_context(tc.tile_pool(name="work", bufs=3))
         psum = ctx.enter_context(tc.psum_pool(name="psum", bufs=2))
 
@@ -120,6 +120,13 @@ def tile_routed_moe_kernel(tc, xT, w1, w3, w2, gate, offs, out):
                     raw[:, b].rearrange("p j (c i) -> p c j i", i=4))
             return grouped
 
+        def load_w2_halves(e):
+            raw = raws.tile([P, B, J * N], F32, name="raw", align_bytes=512)
+            rows = w2[e].rearrange("(b p j) n -> p b (j n)", p=P, j=J)
+            for b in range(B):
+                nc.sync.dma_start(out=raw[:, b], in_=rows[:, b])
+            return raw[:].rearrange("p b (j n) -> p b j n", j=J)
+
         def new_w2():
             codes = weights.tile([P, B, N], U32, name="w2_codes", align_bytes=64)
             scales = weights.tile([P, B, N], U8, name="w2_scales", align_bytes=64)
@@ -171,15 +178,18 @@ def tile_routed_moe_kernel(tc, xT, w1, w3, w2, gate, offs, out):
                                         sig[:, 2 * u:2 * u + 2].rearrange("p t n -> p n t"), MULT)
             return h
 
-        def open_gates(operand, e, b):
+        def open_gates_into(sig, operand, e, b):
             a = hidden_sums(operand, e, b, "a")
-            sig = work.tile([P, J, C], F32, name=f"sig{b}")
-            nc.scalar.activation(sig[:], a[:], SIGMOID)
+            nc.scalar.activation(sig, a[:], SIGMOID)
             return sig
+
+        def open_gates(operand, e, b):
+            sig = work.tile([P, J, C], F32, name=f"sig{b}")
+            return open_gates_into(sig[:], operand, e, b)
 
         def product_into(h, v, sig):
             nc.vector.tensor_tensor(h.rearrange("p (n t) -> p n t", t=J), v[:].rearrange("p t n -> p n t"),
-                                    sig[:].rearrange("p t n -> p n t"), MULT)
+                                    sig.rearrange("p t n -> p n t"), MULT)
             return h
 
         def product(v, sig):
@@ -216,8 +226,9 @@ def tile_routed_moe_kernel(tc, xT, w1, w3, w2, gate, offs, out):
 
         def interleave_whole_w2(raw, engine):
             grouped = groups.tile([P, B, N, J], BF16, name="w2_both", align_bytes=64, bufs=2)
-            copy_on(engine, grouped[:].rearrange("p b (c i) j -> p b c j i", i=4),
-                    raw.rearrange("p b j (c i) -> p b c j i", i=4))
+            for b in range(B):
+                copy_on(engine, grouped[:, b].rearrange("p (c i) j -> p c j i", i=4),
+                        raw[:, b].rearrange("p j (c i) -> p c j i", i=4))
             return grouped
 
         def quantize_both(values, operand):
@@ -248,35 +259,38 @@ def tile_routed_moe_kernel(tc, xT, w1, w3, w2, gate, offs, out):
                     scatter(e, second_sums(prepare_w2(e), h_op, new_y()), gates[:, e * C:(e + 1) * C])
         whole_pass(w1[e], op1, 0, (P, 0))
         whole_pass(w1[e], op1, 1, (88, 56))
-        sigs = [open_gates(op1, e, 0)]
+        last = keep.tile([P, PASS * J + 2 * PASS], BF16, name="last_block", align_bytes=64)
+        first_sig = last[:, PASS * J - 32:PASS * J - 32 + 2 * PASS].bitcast(F32).rearrange("p (t n) -> p t n", t=J)
+        sigs = [open_gates_into(first_sig, op1, e, 0)]
         raw_1 = load_columns(w3[e], 0, 0, PASS)
         raw_2 = load_columns(w3[e], 1, 0, PASS)
         raw_3 = load_columns(w3[e], 0, PASS, H)
         raw_4 = load_columns(w3[e], 1, PASS, PASS + J * 64)
         raw_5 = load_columns(w3[e], 1, PASS + J * 64, H)
-        raw_c, op_c = load_w2(e - 1), new_w2()
-        raw_d, op_d = load_w2(e), new_w2()
-        late_gates = raws.tile([P, 2 * C], F32, name="raw", align_bytes=512)
+        raw_c, op_c = load_w2_halves(e - 1), new_w2()
+        raw_d, op_d = load_w2_halves(e), new_w2()
+        late_gates = keep.tile([P, 2 * C], F32, name="late_gates", align_bytes=512)
         nc.sync.dma_start(late_gates[:], gate[:, 2 * C:])
         quantize_pass(block(raw_1, 0, 0, 64), op3, 0, 0, 1)
-        quantize_pass(block(raw_2, 0, 0, 64), op3, 1, 0, 1)
-        sigs.append(open_gates(op1, e, 1))
+        quantize_pass(block(raw_2, 0, 0, 76), op3, 1, 0, 4)
+        second_sig = raw_2.rearrange("p j c -> p (j c)")[:, :PASS].rearrange("p (t n) -> p t n", t=J)
+        sigs.append(open_gates_into(second_sig, op1, e, 1))
         v0 = hidden_sums(op3, e, 0, "v")
         quantize_pass(block(raw_3, 0, 1, 64), op3, 0, 1, 1)
-        h0 = product(v0, sigs[0])
-        grouped_b = groups.tile([P, PASS * J], BF16, name="grouped1", align_bytes=64)
+        h0 = product_into(raw_3.rearrange("p j c -> p (j c)")[:, :PASS // 2].bitcast(BF16), v0, sigs[0])
+        quantize_hidden(h0, h_op, 0)
+        grouped_b = last[:, :PASS * J]
         interleave(1, grouped_b, raw_4, 0, 0, 64)
-        interleave(0, grouped_b, raw_5, -J * 64, 64, 104)
-        interleave(1, grouped_b, raw_5, -J * 64, 104, P)
+        interleave(1, grouped_b, raw_5, -J * 64, 64, 88)
+        interleave(0, grouped_b, raw_5, -J * 64, 88, P)
         quantize_pass(grouped_b, op3, 1, 1, 4)
         v1 = paired_sums(op3, e, 1)
         both_c = interleave_whole_w2(raw_c, 1)
         both_d = interleave_whole_w2(raw_d, 1)
         values_c = both_c[:].rearrange("p b n j -> p (b n j)")
         quantize_both(values_c, op_c)
-        y_c = second_sums(op_c, h_ops[e - 1], raw_d[:, 0, 0])
-        h1 = paired_product(raw_c.rearrange("p b j n -> p (b j n)")[:, 0:PASS // 2].bitcast(BF16), v1, sigs[1])
-        quantize_hidden(h0, h_op, 0)
+        y_c = second_sums(op_c, h_ops[e - 1], raw_d[:, 1, 0])
+        h1 = paired_product(raw_c.rearrange("p b j n -> p (b j n)")[:, PASS:PASS + PASS // 2].bitcast(BF16), v1, sigs[1])
         quantize_both(both_d[:].rearrange("p b n j -> p (b n j)"), op_d)
         quantize_hidden(h1, h_op, 1)
         y_d = second_sums(op_d, h_op, new_y())

@@ -109,19 +109,13 @@ def tile_routed_moe_kernel(tc, xT, w1, w3, w2, gate, offs, out):
             for b in range(B):
                 quantize_pass(blocks[b], operand, g, b, 1)
 
-        def load_w2(e):
-            raw = raws.tile([P, B, J * N], F32, name="raw", align_bytes=512)
-            nc.sync.dma_start(out=raw[:], in_=w2[e].rearrange("(b p j) n -> p b (j n)", p=P, j=J))
-            return raw[:].rearrange("p b (j n) -> p b j n", j=J)
-
         def interleave_w2(raw, b, engine):
             grouped = groups.tile([P, N, J], BF16, name=f"w2_grouped{b}", align_bytes=64)
             copy_on(engine, grouped[:].rearrange("p (c i) j -> p c j i", i=4),
                     raw[:, b].rearrange("p j (c i) -> p c j i", i=4))
             return grouped
 
-        def load_w2_halves(e):
-            raw = raws.tile([P, B, J * N], F32, name="raw", align_bytes=512)
+        def load_w2_halves(e, raw):
             rows = w2[e].rearrange("(b p j) n -> p b (j n)", p=P, j=J)
             for b in range(B):
                 nc.sync.dma_start(out=raw[:, b], in_=rows[:, b])
@@ -137,7 +131,8 @@ def tile_routed_moe_kernel(tc, xT, w1, w3, w2, gate, offs, out):
                                   in_=grouped[:].rearrange("p n j -> p (n j)"))
 
         def prepare_w2(e):
-            raw, operand = load_w2(e), new_w2()
+            landing = keep.tile([P, B, J * N], F32, name=f"w2_raw{e}", align_bytes=512)
+            raw, operand = load_w2_halves(e, landing), new_w2()
             blocks = [interleave_w2(raw, b, b) for b in range(B)]
             for b in range(B):
                 quantize_w2(blocks[b], operand, b)
@@ -267,8 +262,10 @@ def tile_routed_moe_kernel(tc, xT, w1, w3, w2, gate, offs, out):
         raw_3 = load_columns(w3[e], 0, PASS, H)
         raw_4 = load_columns(w3[e], 1, PASS, PASS + J * 64)
         raw_5 = load_columns(w3[e], 1, PASS + J * 64, H)
-        raw_c, op_c = load_w2_halves(e - 1), new_w2()
-        raw_d, op_d = load_w2_halves(e), new_w2()
+        landing_c = raws.tile([P, B, J * N], F32, name="raw", align_bytes=512)
+        raw_c, op_c = load_w2_halves(e - 1, landing_c), new_w2()
+        landing_d = raws.tile([P, B, J * N], F32, name="raw", align_bytes=512)
+        raw_d, op_d = load_w2_halves(e, landing_d), new_w2()
         late_gates = keep.tile([P, 2 * C], F32, name="late_gates", align_bytes=512)
         nc.sync.dma_start(late_gates[:], gate[:, 2 * C:])
         quantize_pass(block(raw_1, 0, 0, 64), op3, 0, 0, 1)
@@ -287,8 +284,8 @@ def tile_routed_moe_kernel(tc, xT, w1, w3, w2, gate, offs, out):
         v1 = paired_sums(op3, e, 1)
         both_c = interleave_whole_w2(raw_c, 1)
         both_d = interleave_whole_w2(raw_d, 1)
-        values_c = both_c[:].rearrange("p b n j -> p (b n j)")
-        quantize_both(values_c, op_c)
+        for b in range(B):
+            quantize_w2(both_c[:, b], op_c, b)
         y_c = second_sums(op_c, h_ops[e - 1], raw_d[:, 1, 0])
         h1 = paired_product(raw_c.rearrange("p b j n -> p (b j n)")[:, PASS:PASS + PASS // 2].bitcast(BF16), v1, sigs[1])
         quantize_both(both_d[:].rearrange("p b n j -> p (b n j)"), op_d)

@@ -109,12 +109,6 @@ def tile_routed_moe_kernel(tc, xT, w1, w3, w2, gate, offs, out):
             for b in range(B):
                 quantize_pass(blocks[b], operand, g, b, 1)
 
-        def interleave_w2(raw, b, engine):
-            grouped = groups.tile([P, N, J], BF16, name=f"w2_grouped{b}", align_bytes=64)
-            copy_on(engine, grouped[:].rearrange("p (c i) j -> p c j i", i=4),
-                    raw[:, b].rearrange("p j (c i) -> p c j i", i=4))
-            return grouped
-
         def load_w2_halves(e, raw):
             rows = w2[e].rearrange("(b p j) n -> p b (j n)", p=P, j=J)
             for b in range(B):
@@ -130,12 +124,19 @@ def tile_routed_moe_kernel(tc, xT, w1, w3, w2, gate, offs, out):
             nc.vector.quantize_mx(out=operand[0][:, b].bitcast(FP8X4), scales=operand[1][:, b],
                                   in_=grouped[:].rearrange("p n j -> p (n j)"))
 
+        def load_early_w2():
+            raw = raws.tile([P, (E - 2) * B, J * N], F32, name="raw", align_bytes=512)
+            nc.sync.dma_start(out=raw[:], in_=w2[:E - 2].rearrange("e (b p j) n -> p (e b) (j n)", p=P, j=J))
+            grouped = keep.tile([P, (E - 2) * B, N, J], BF16, name="early_w2", align_bytes=64)
+            for i in range((E - 2) * B):
+                copy_on(i % 2, grouped[:, i].rearrange("p (c i) j -> p c j i", i=4),
+                        raw[:, i].rearrange("p (j c i) -> p c j i", j=J, i=4))
+            return grouped
+
         def prepare_w2(e):
-            landing = keep.tile([P, B, J * N], F32, name=f"w2_raw{e}", align_bytes=512)
-            raw, operand = load_w2_halves(e, landing), new_w2()
-            blocks = [interleave_w2(raw, b, b) for b in range(B)]
+            operand = new_w2()
             for b in range(B):
-                quantize_w2(blocks[b], operand, b)
+                quantize_w2(early_w2[:, e * B + b], operand, b)
             return operand
 
         def hidden_sums(operand, e, b, name):
@@ -195,7 +196,7 @@ def tile_routed_moe_kernel(tc, xT, w1, w3, w2, gate, offs, out):
             nc.vector.quantize_mx(out=h_operand[0][:, b, :].bitcast(FP8X4), scales=h_operand[1][:, b, :],
                                   in_=h)
 
-        def second_sums(w2_operand, h_operand, y_sb):
+        def second_sums(w2_operand, h_operand):
             y = psum.tile([N, C], F32, name="y")
             for b in range(B):
                 nc.tensor.matmul_mx(
@@ -203,6 +204,9 @@ def tile_routed_moe_kernel(tc, xT, w1, w3, w2, gate, offs, out):
                     lhsT=w2_operand[0][:, b, :].bitcast(FP8X4), lhsT_scale=w2_operand[1][:, b, :],
                     rhs=h_operand[0][:, b, :].bitcast(FP8X4), rhs_scale=h_operand[1][:, b, :],
                     start=(b == 0), stop=(b == B - 1))
+            return y
+
+        def leave_psum(y, y_sb):
             nc.scalar.copy(y_sb, y[:])
             return y_sb
 
@@ -248,10 +252,11 @@ def tile_routed_moe_kernel(tc, xT, w1, w3, w2, gate, offs, out):
                     whole_pass(w3[e], op3, g, (P, 0))
                 if e == 0:
                     nc.sync.dma_start(gates[:], gate[:, :2 * C])
+                    early_w2 = load_early_w2()
                 for b in range(B):
                     quantize_hidden(product(hidden_sums(op3, e, b, "v"), sigs[b]), h_op, b)
                 if e < E - 2:
-                    scatter(e, second_sums(prepare_w2(e), h_op, new_y()), gates[:, e * C:(e + 1) * C])
+                    scatter(e, leave_psum(second_sums(prepare_w2(e), h_op), new_y()), gates[:, e * C:(e + 1) * C])
         whole_pass(w1[e], op1, 0, (P, 0))
         whole_pass(w1[e], op1, 1, (88, 56))
         last = keep.tile([P, PASS * J + 2 * PASS], BF16, name="last_block", align_bytes=64)
@@ -286,11 +291,13 @@ def tile_routed_moe_kernel(tc, xT, w1, w3, w2, gate, offs, out):
         both_d = interleave_whole_w2(raw_d, 1)
         for b in range(B):
             quantize_w2(both_c[:, b], op_c, b)
-        y_c = second_sums(op_c, h_ops[e - 1], raw_d[:, 1, 0])
+        y_c = leave_psum(second_sums(op_c, h_ops[e - 1]), raw_d[:, 1, 0])
         h1 = paired_product(raw_c.rearrange("p b j n -> p (b j n)")[:, PASS:PASS + PASS // 2].bitcast(BF16), v1, sigs[1])
         quantize_both(both_d[:].rearrange("p b n j -> p (b n j)"), op_d)
         quantize_hidden(h1, h_op, 1)
-        y_d = second_sums(op_d, h_op, new_y())
+        y_d = second_sums(op_d, h_op)
         scatter(e - 1, y_c, late_gates[:, :C])
-        scatter(e, y_d, late_gates[:, C:])
+        gated = new_y()
+        nc.vector.tensor_tensor(gated, y_d[:], late_gates[:, C:], MULT)
+        nc.vector.tensor_copy(window[:].indirect(offsets[:, e * (C // 16):]), gated)
         nc.sync.dma_start(out, window[:])

@@ -171,21 +171,21 @@ def tile_routed_moe_kernel(tc, xT, w1, w3, w2, gate, offs, out):
             for u in range(2):
                 nc.vector.tensor_tensor(h.rearrange("p (n t) -> p n t", t=J)[:, :, 2 * u:2 * u + 2],
                                         banks[u][:].rearrange("p t n -> p n t"),
-                                        sig[:, 2 * u:2 * u + 2].rearrange("p t n -> p n t"), MULT)
+                                        sig[:, :, 2 * u:2 * u + 2], MULT)
             return h
 
         def open_gates_into(sig, operand, e, b):
             a = hidden_sums(operand, e, b, "a")
-            nc.scalar.activation(sig, a[:], SIGMOID)
+            nc.scalar.activation(sig, a[:].rearrange("p t n -> p n t"), SIGMOID)
             return sig
 
         def open_gates(operand, e, b):
-            sig = work.tile([P, J, C], F32, name=f"sig{b}")
+            sig = work.tile([P, C, J], F32, name=f"sig{b}")
             return open_gates_into(sig[:], operand, e, b)
 
         def product_into(h, v, sig):
             nc.vector.tensor_tensor(h.rearrange("p (n t) -> p n t", t=J), v[:].rearrange("p t n -> p n t"),
-                                    sig.rearrange("p t n -> p n t"), MULT)
+                                    sig, MULT)
             return h
 
         def product(v, sig):
@@ -230,10 +230,6 @@ def tile_routed_moe_kernel(tc, xT, w1, w3, w2, gate, offs, out):
                         raw[:, b].rearrange("p j (c i) -> p c j i", i=4))
             return grouped
 
-        def quantize_both(values, operand):
-            nc.vector.quantize_mx(out=operand[0][:].rearrange("p b n -> p (b n)").bitcast(FP8X4),
-                                  scales=operand[1][:].rearrange("p b n -> p (b n)"), in_=values)
-
         def load_columns(dram, g, c0, c1):
             raw = raws.tile([P, J, c1 - c0], F32, name="raw", align_bytes=512)
             rows = dram.rearrange("(g p j) c -> g p j c", p=P, j=J)[g]
@@ -260,7 +256,7 @@ def tile_routed_moe_kernel(tc, xT, w1, w3, w2, gate, offs, out):
         whole_pass(w1[e], op1, 0, (P, 0))
         whole_pass(w1[e], op1, 1, (88, 56))
         last = keep.tile([P, PASS * J + 2 * PASS], BF16, name="last_block", align_bytes=64)
-        first_sig = last[:, PASS * J - 32:PASS * J - 32 + 2 * PASS].bitcast(F32).rearrange("p (t n) -> p t n", t=J)
+        first_sig = last[:, PASS * J - 32:PASS * J - 32 + 2 * PASS].bitcast(F32).rearrange("p (n t) -> p n t", t=J)
         sigs = [open_gates_into(first_sig, op1, e, 0)]
         raw_1 = load_columns(w3[e], 0, 0, PASS)
         raw_2 = load_columns(w3[e], 1, 0, PASS)
@@ -275,7 +271,7 @@ def tile_routed_moe_kernel(tc, xT, w1, w3, w2, gate, offs, out):
         nc.sync.dma_start(late_gates[:], gate[:, 2 * C:])
         quantize_pass(block(raw_1, 0, 0, 64), op3, 0, 0, 1)
         quantize_pass(block(raw_2, 0, 0, 76), op3, 1, 0, 4)
-        second_sig = raw_2.rearrange("p j c -> p (j c)")[:, :PASS].rearrange("p (t n) -> p t n", t=J)
+        second_sig = raw_2.rearrange("p j c -> p (j c)")[:, :PASS].rearrange("p (n t) -> p n t", t=J)
         sigs.append(open_gates_into(second_sig, op1, e, 1))
         v0 = hidden_sums(op3, e, 0, "v")
         quantize_pass(block(raw_3, 0, 1, 64), op3, 0, 1, 1)
@@ -293,8 +289,9 @@ def tile_routed_moe_kernel(tc, xT, w1, w3, w2, gate, offs, out):
             quantize_w2(both_c[:, b], op_c, b)
         y_c = leave_psum(second_sums(op_c, h_ops[e - 1]), raw_d[:, 1, 0])
         h1 = paired_product(raw_c.rearrange("p b j n -> p (b j n)")[:, PASS:PASS + PASS // 2].bitcast(BF16), v1, sigs[1])
-        quantize_both(both_d[:].rearrange("p b n j -> p (b n j)"), op_d)
+        quantize_w2(both_d[:, 0], op_d, 0)
         quantize_hidden(h1, h_op, 1)
+        quantize_w2(both_d[:, 1], op_d, 1)
         y_d = second_sums(op_d, h_op)
         scatter(e - 1, y_c, late_gates[:, :C])
         gated = new_y()

@@ -32,8 +32,6 @@ def tile_routed_moe_kernel(tc, xT, w1, w3, w2, gate, offs, out):
         work = ctx.enter_context(tc.tile_pool(name="work", bufs=3))
         psum = ctx.enter_context(tc.psum_pool(name="psum", bufs=2))
 
-        pairs = ctx.enter_context(tc.psum_pool(name="pairs", bufs=1))
-
         offsets = keep.tile([P, E * C // 16], U16, name="offsets")
         gates = keep.tile([P, 2 * C], F32, name="gates", align_bytes=512)
         window = keep.tile([P, T], F32, name="window", align_bytes=512)
@@ -153,26 +151,19 @@ def tile_routed_moe_kernel(tc, xT, w1, w3, w2, gate, offs, out):
                         start=(g == 0), stop=(g == G - 1))
             return acc
 
-        def paired_sums(operand, e, b):
+        def grouped_sums(operand, e, b):
             codes, scales = operand
+            acc = psum.tile([P, J, C], F32, name="v")
             slots = slice(e * C, (e + 1) * C)
-            banks = [pairs.tile([P, 2, C], F32, name=f"pair{u}") for u in range(2)]
-            for t in range(J):
-                cols = slice(b * PASS + t * P, b * PASS + (t + 1) * P)
-                for g in range(G):
+            for g in range(G):
+                for t in range(J):
+                    cols = slice(b * PASS + t * P, b * PASS + (t + 1) * P)
                     nc.tensor.matmul_mx(
-                        out=banks[t // 2][:, t % 2, :],
+                        out=acc[:, t, :],
                         lhsT=codes[:, g, cols].bitcast(FP8X4), lhsT_scale=scales[:, g, cols],
                         rhs=slot_codes[:, g, slots].bitcast(FP8X4), rhs_scale=slot_scales[:, g, slots],
-                        start=(g == 0), stop=(g == G - 1))
-            return banks
-
-        def paired_product(h, banks, sig):
-            for u in range(2):
-                nc.vector.tensor_tensor(h.rearrange("p (n t) -> p n t", t=J)[:, :, 2 * u:2 * u + 2],
-                                        banks[u][:].rearrange("p t n -> p n t"),
-                                        sig[:, :, 2 * u:2 * u + 2], MULT)
-            return h
+                        start=(g == 0 and t == 0), stop=(g == G - 1 and t == J - 1))
+            return acc
 
         def open_gates_into(sig, operand, e, b):
             a = hidden_sums(operand, e, b, "a")
@@ -282,18 +273,20 @@ def tile_routed_moe_kernel(tc, xT, w1, w3, w2, gate, offs, out):
         interleave(1, grouped_b, raw_5, -J * 64, 64, 88)
         interleave(0, grouped_b, raw_5, -J * 64, 88, P)
         quantize_pass(grouped_b, op3, 1, 1, 4)
-        v1 = paired_sums(op3, e, 1)
+        v1 = grouped_sums(op3, e, 1)
         both_c = interleave_whole_w2(raw_c, 1)
         both_d = interleave_whole_w2(raw_d, 1)
         for b in range(B):
             quantize_w2(both_c[:, b], op_c, b)
-        y_c = leave_psum(second_sums(op_c, h_ops[e - 1]), raw_d[:, 1, 0])
-        h1 = paired_product(raw_c.rearrange("p b j n -> p (b j n)")[:, PASS:PASS + PASS // 2].bitcast(BF16), v1, sigs[1])
+        y_c = second_sums(op_c, h_ops[e - 1])
+        h1 = product_into(raw_c.rearrange("p b j n -> p (b j n)")[:, PASS:PASS + PASS // 2].bitcast(BF16), v1, sigs[1])
         quantize_w2(both_d[:, 0], op_d, 0)
+        gated_c = second_sig.rearrange("p n t -> p (n t)")[:, PASS - C:]
+        nc.vector.tensor_tensor(gated_c, y_c[:], late_gates[:, :C], MULT)
         quantize_hidden(h1, h_op, 1)
         quantize_w2(both_d[:, 1], op_d, 1)
         y_d = second_sums(op_d, h_op)
-        scatter(e - 1, y_c, late_gates[:, :C])
+        nc.vector.tensor_copy(window[:].indirect(offsets[:, (e - 1) * (C // 16):e * (C // 16)]), gated_c)
         gated = new_y()
         nc.vector.tensor_tensor(gated, y_d[:], late_gates[:, C:], MULT)
         nc.vector.tensor_copy(window[:].indirect(offsets[:, e * (C // 16):]), gated)

@@ -75,8 +75,8 @@ def tile_routed_moe_kernel(tc, xT, w1, w3, w2, gate, offs, out):
             return raw[:].rearrange("p (j c) -> p j c", j=J)
 
         def interleave(engine, grouped, raw, c0, m0, m1):
-            copy_on(engine, grouped[:].rearrange("p (u v m j) -> p u m j v", u=2, v=2, j=J)[:, :, m0:m1],
-                    raw[:, :, c0 + J * m0:c0 + J * m1].rearrange("p j (m u v) -> p u m j v", u=2, v=2))
+            copy_on(engine, grouped[:].rearrange("p (t m j) -> p m j t", t=J, j=J)[:, m0:m1],
+                    raw[:, :, c0 + J * m0:c0 + J * m1].rearrange("p j (m t) -> p m j t", t=J))
 
         def quantize(grouped, codes, scales, c0, parts):
             width = PASS // parts

@@ -13,6 +13,7 @@ U8 = mybir.dt.uint8
 FP8X4 = mybir.dt.float8_e4m3fn_x4
 MULT = mybir.AluOpType.mult
 SIGMOID = mybir.ActivationFunctionType.Sigmoid
+COPY = mybir.ActivationFunctionType.Copy
 
 P = 128
 J = 4
@@ -286,7 +287,7 @@ def tile_routed_moe_kernel(tc, xT, w1, w3, w2, gate, offs, out):
         quantize_hidden(h1, h_op, 1)
         quantize_w2(both_d[:, 1], op_d, 1)
         y_d = second_sums(op_d, h_op)
-        nc.vector.tensor_copy(window[:].indirect(offsets[:, (e - 1) * (C // 16):e * (C // 16)]), gated_c)
+        nc.scalar.activation(window[:].indirect(offsets[:, (e - 1) * (C // 16):e * (C // 16)]), gated_c, COPY)
         gated = new_y()
         nc.vector.tensor_tensor(gated, y_d[:], late_gates[:, C:], MULT)
         nc.vector.tensor_copy(window[:].indirect(offsets[:, e * (C // 16):]), gated)

@@ -253,8 +253,11 @@ def tile_routed_moe_kernel(tc, xT, w1, w3, w2, gate, offs, out):
         raw_1 = load_columns(w3[e], 0, 0, PASS)
         raw_2 = load_columns(w3[e], 1, 0, PASS)
         raw_3 = load_columns(w3[e], 0, PASS, H)
-        raw_4 = load_columns(w3[e], 1, PASS, PASS + J * 64)
-        raw_5 = load_columns(w3[e], 1, PASS + J * 64, H)
+        landing_b = raws.tile([P, J, PASS], F32, name="raw", align_bytes=512)
+        raw_b = landing_b[:]
+        for c0 in (0, PASS // 2):
+            nc.sync.dma_start(out=raw_b[:, :, c0:c0 + PASS // 2],
+                              in_=w3[e].rearrange("(g p j) c -> g p j c", p=P, j=J)[1][:, :, PASS + c0:PASS + c0 + PASS // 2])
         landing_c = raws.tile([P, B, J * N], F32, name="raw", align_bytes=512)
         raw_c, op_c = load_w2_halves(e - 1, landing_c), new_w2()
         landing_d = raws.tile([P, B, J * N], F32, name="raw", align_bytes=512)
@@ -270,10 +273,16 @@ def tile_routed_moe_kernel(tc, xT, w1, w3, w2, gate, offs, out):
         h0 = product_into(raw_3.rearrange("p j c -> p (j c)")[:, :PASS // 2].bitcast(BF16), v0, sigs[0])
         quantize_hidden(h0, h_op, 0)
         grouped_b = last[:, :PASS * J]
-        interleave(1, grouped_b, raw_4, 0, 0, 64)
-        interleave(1, grouped_b, raw_5, -J * 64, 64, 88)
-        interleave(0, grouped_b, raw_5, -J * 64, 88, P)
-        quantize_pass(grouped_b, op3, 1, 1, 4)
+        interleave(1, grouped_b, raw_b, 0, 0, 60)
+        interleave(0, grouped_b, raw_b, 0, 60, 68)
+        interleave(1, grouped_b, raw_b, 0, 68, 96)
+        interleave(0, grouped_b, raw_b, 0, 96, P)
+        for half in range(2):
+            for t in range(J):
+                first = t * P + half * (P // 2)
+                cols = slice(PASS + first, PASS + first + P // 2)
+                nc.vector.quantize_mx(out=op3[0][:, 1, cols].bitcast(FP8X4), scales=op3[1][:, 1, cols],
+                                      in_=grouped_b[:, first * J:(first + P // 2) * J])
         v1 = grouped_sums(op3, e, 1)
         both_c = interleave_whole_w2(raw_c, 1)
         both_d = interleave_whole_w2(raw_d, 1)

from contextlib import ExitStack

import concourse.mybir as mybir

K, T, E, C, H, N = 1024, 512, 4, 128, 1024, 128
FLOPS = 2 * E * C * (2 * K * H + H * N)

F32 = mybir.dt.float32
BF16 = mybir.dt.bfloat16
U32 = mybir.dt.uint32
U16 = mybir.dt.uint16
U8 = mybir.dt.uint8
FP8X4 = mybir.dt.float8_e4m3fn_x4
MULT = mybir.AluOpType.mult
SIGMOID = mybir.ActivationFunctionType.Sigmoid
COPY = mybir.ActivationFunctionType.Copy

P = 128
J = 4
PASS = P * J
G = K // PASS
B = H // PASS


def tile_routed_moe_kernel(tc, xT, w1, w3, w2, gate, offs, out):
    nc = tc.nc

    with ExitStack() as ctx:
        keep = ctx.enter_context(tc.tile_pool(name="keep", bufs=1))
        raws = ctx.enter_context(tc.tile_pool(name="raws", bufs=6))
        groups = ctx.enter_context(tc.tile_pool(name="groups", bufs=3))
        weights = ctx.enter_context(tc.tile_pool(name="weights", bufs=2))
        work = ctx.enter_context(tc.tile_pool(name="work", bufs=3))
        psum = ctx.enter_context(tc.psum_pool(name="psum", bufs=2))

        offsets = keep.tile([P, E * C // 16], U16, name="offsets")
        gates = keep.tile([P, 2 * C], F32, name="gates", align_bytes=512)
        window = keep.tile([P, T], F32, name="window", align_bytes=512)
        slot_codes = keep.tile([P, G, E * C], U32, name="slot_codes", align_bytes=64)
        slot_scales = keep.tile([P, G, E * C], U8, name="slot_scales", align_bytes=64)

        def copy_on(engine, dst, src):
            if engine == 0:
                nc.vector.tensor_copy(dst, src)
            else:
                nc.scalar.copy(dst, src)

        token_codes, token_scales, token_raw = [], [], []
        for g in range(G):
            codes = keep.tile([P, T], U32, name=f"token_codes{g}", align_bytes=64)
            scales = keep.tile([P, T], U8, name=f"token_scales{g}", align_bytes=64)
            nc.gpsimd.memset(scales[:], 0)
            token_codes.append(codes)
            token_scales.append(scales)
            raw = raws.tile([P, J * T], F32, name="raw", align_bytes=512)
            nc.sync.dma_start(out=raw[:], in_=xT.rearrange("(g p j) n -> g p (j n)", p=P, j=J)[g])
            token_raw.append(raw[:].rearrange("p (j n) -> p j n", j=J))
            if g == 0:
                nc.sync.dma_start(offsets[:], offs)
        for g in range(G):
            grouped = keep.tile([P, T, J], BF16, name=f"token_grouped{g}", align_bytes=64)
            copy_on(g, grouped[:].rearrange("p (c i) j -> p c j i", i=4),
                    token_raw[g].rearrange("p j (c i) -> p c j i", i=4))
            nc.vector.quantize_mx(out=token_codes[g][:].bitcast(FP8X4), scales=token_scales[g][:],
                                  in_=grouped[:].rearrange("p n j -> p (n j)"))
        piece = 256
        for s in range(E * C // piece):
            cols = offsets[:, s * (piece // 16):(s + 1) * (piece // 16)]
            for g in range(G):
                nc.vector.tensor_copy(slot_codes[:, g, s * piece:(s + 1) * piece], token_codes[g][:].indirect(cols))
                nc.vector.tensor_copy(slot_scales[:, g, s * piece:(s + 1) * piece], token_scales[g][:].indirect(cols))

        def load_pass(dram, g):
            raw = raws.tile([P, J * H], F32, name="raw", align_bytes=512)
            nc.sync.dma_start(out=raw[:], in_=dram.rearrange("(g p j) c -> g p (j c)", p=P, j=J)[g])
            return raw[:].rearrange("p (j c) -> p j c", j=J)

        def interleave(engine, grouped, raw, c0, m0, m1):
            copy_on(engine, grouped[:].rearrange("p (t m j) -> p m j t", t=J, j=J)[:, m0:m1],
                    raw[:, :, c0 + J * m0:c0 + J * m1].rearrange("p j (m t) -> p m j t", t=J))

        def quantize(grouped, codes, scales, c0, parts):
            width = PASS // parts
            for i in range(parts):
                cols = slice(c0 + i * width, c0 + (i + 1) * width)
                nc.vector.quantize_mx(out=codes[:, cols].bitcast(FP8X4), scales=scales[:, cols],
                                      in_=grouped[:, i * width * J:(i + 1) * width * J])

        def new_operand(name):
            codes = weights.tile([P, G, H], U32, name=f"{name}_codes", align_bytes=64)
            scales = weights.tile([P, G, H], U8, name=f"{name}_scales", align_bytes=64)
            return codes, scales

        def block(raw, c0, b, cut):
            grouped = groups.tile([P, PASS * J], BF16, name=f"grouped{b}", align_bytes=64)
            if cut > 0:
                interleave(0, grouped, raw, c0, 0, cut)
            if cut < P:
                interleave(1, grouped, raw, c0, cut, P)
            return grouped

        def quantize_pass(grouped, operand, g, b, parts):
            quantize(grouped, operand[0][:, g], operand[1][:, g], b * PASS, parts)

        def whole_pass(dram, operand, g, cuts):
            raw = load_pass(dram, g)
            blocks = [block(raw, b * PASS, b, cuts[b]) for b in range(B)]
            for b in range(B):
                quantize_pass(blocks[b], operand, g, b, 1)

        def load_w2_halves(e, raw):
            rows = w2[e].rearrange("(b p j) n -> p b (j n)", p=P, j=J)
            for b in range(B):
                nc.sync.dma_start(out=raw[:, b], in_=rows[:, b])
            return raw[:].rearrange("p b (j n) -> p b j n", j=J)

        def new_w2():
            codes = weights.tile([P, B, N], U32, name="w2_codes", align_bytes=64)
            scales = weights.tile([P, B, N], U8, name="w2_scales", align_bytes=64)
            return codes, scales

        def quantize_w2(grouped, operand, b):
            nc.vector.quantize_mx(out=operand[0][:, b].bitcast(FP8X4), scales=operand[1][:, b],
                                  in_=grouped[:].rearrange("p n j -> p (n j)"))

        def load_early_w2():
            raw = raws.tile([P, (E - 2) * B, J * N], F32, name="raw", align_bytes=512)
            nc.sync.dma_start(out=raw[:], in_=w2[:E - 2].rearrange("e (b p j) n -> p (e b) (j n)", p=P, j=J))
            grouped = keep.tile([P, (E - 2) * B, N, J], BF16, name="early_w2", align_bytes=64)
            for i in range((E - 2) * B):
                copy_on(i % 2, grouped[:, i].rearrange("p (c i) j -> p c j i", i=4),
                        raw[:, i].rearrange("p (j c i) -> p c j i", j=J, i=4))
            return grouped

        def prepare_w2(e):
            operand = new_w2()
            for b in range(B):
                quantize_w2(early_w2[:, e * B + b], operand, b)
            return operand

        def hidden_sums(operand, e, b, name):
            codes, scales = operand
            acc = psum.tile([P, J, C], F32, name=name)
            slots = slice(e * C, (e + 1) * C)
            for t in range(J):
                cols = slice(b * PASS + t * P, b * PASS + (t + 1) * P)
                for g in range(G):
                    nc.tensor.matmul_mx(
                        out=acc[:, t, :],
                        lhsT=codes[:, g, cols].bitcast(FP8X4), lhsT_scale=scales[:, g, cols],
                        rhs=slot_codes[:, g, slots].bitcast(FP8X4), rhs_scale=slot_scales[:, g, slots],
                        start=(g == 0), stop=(g == G - 1))
            return acc

        def grouped_sums(operand, e, b):
            codes, scales = operand
            acc = psum.tile([P, J, C], F32, name="v")
            slots = slice(e * C, (e + 1) * C)
            for g in range(G):
                for t in range(J):
                    cols = slice(b * PASS + t * P, b * PASS + (t + 1) * P)
                    nc.tensor.matmul_mx(
                        out=acc[:, t, :],
                        lhsT=codes[:, g, cols].bitcast(FP8X4), lhsT_scale=scales[:, g, cols],
                        rhs=slot_codes[:, g, slots].bitcast(FP8X4), rhs_scale=slot_scales[:, g, slots],
                        start=(g == 0 and t == 0), stop=(g == G - 1 and t == J - 1))
            return acc

        def open_gates_into(sig, operand, e, b):
            a = hidden_sums(operand, e, b, "a")
            nc.scalar.activation(sig, a[:].rearrange("p t n -> p n t"), SIGMOID)
            return sig

        def open_gates(operand, e, b):
            sig = work.tile([P, C, J], F32, name=f"sig{b}")
            return open_gates_into(sig[:], operand, e, b)

        def product_into(h, v, sig):
            nc.vector.tensor_tensor(h.rearrange("p (n t) -> p n t", t=J), v[:].rearrange("p t n -> p n t"),
                                    sig, MULT)
            return h

        def product(v, sig):
            h = work.tile([P, C * J], BF16, name="h", align_bytes=64)
            return product_into(h[:], v, sig)

        def quantize_hidden(h, h_operand, b):
            nc.vector.quantize_mx(out=h_operand[0][:, b, :].bitcast(FP8X4), scales=h_operand[1][:, b, :],
                                  in_=h)

        def second_sums(w2_operand, h_operand):
            y = psum.tile([N, C], F32, name="y")
            for b in range(B):
                nc.tensor.matmul_mx(
                    out=y[:],
                    lhsT=w2_operand[0][:, b, :].bitcast(FP8X4), lhsT_scale=w2_operand[1][:, b, :],
                    rhs=h_operand[0][:, b, :].bitcast(FP8X4), rhs_scale=h_operand[1][:, b, :],
                    start=(b == 0), stop=(b == B - 1))
            return y

        def leave_psum(y, y_sb):
            nc.scalar.copy(y_sb, y[:])
            return y_sb

        def new_y():
            y_sb = work.tile([N, C], F32, name="y_sb")
            return y_sb[:]

        def scatter(e, y_sb, weight):
            nc.vector.tensor_tensor(window[:].indirect(offsets[:, e * (C // 16):(e + 1) * (C // 16)]),
                                    y_sb, weight, MULT)

        def new_hidden(e):
            codes = keep.tile([P, B, C], U32, name=f"h_codes{e}", align_bytes=64)
            scales = keep.tile([P, B, C], U8, name=f"h_scales{e}", align_bytes=64)
            return codes, scales

        def interleave_whole_w2(raw, engine):
            grouped = groups.tile([P, B, N, J], BF16, name="w2_both", align_bytes=64, bufs=2)
            for b in range(B):
                copy_on(engine, grouped[:, b].rearrange("p (c i) j -> p c j i", i=4),
                        raw[:, b].rearrange("p j (c i) -> p c j i", i=4))
            return grouped

        def load_columns(dram, g, c0, c1):
            raw = raws.tile([P, J, c1 - c0], F32, name="raw", align_bytes=512)
            rows = dram.rearrange("(g p j) c -> g p j c", p=P, j=J)[g]
            nc.sync.dma_start(out=raw[:], in_=rows[:, :, c0:c1])
            return raw[:]

        h_ops = []
        for e in range(E):
            op1, op3, h_op = new_operand("w1"), new_operand("w3"), new_hidden(e)
            h_ops.append(h_op)
            if e < E - 1:
                for g in range(G):
                    whole_pass(w1[e], op1, g, (P, 0))
                sigs = [open_gates(op1, e, b) for b in range(B)]
                for g in range(G):
                    whole_pass(w3[e], op3, g, (P, 0))
                if e == 0:
                    nc.sync.dma_start(gates[:], gate[:, :2 * C])
                    early_w2 = load_early_w2()
                for b in range(B):
                    quantize_hidden(product(hidden_sums(op3, e, b, "v"), sigs[b]), h_op, b)
                if e < E - 2:
                    scatter(e, leave_psum(second_sums(prepare_w2(e), h_op), new_y()), gates[:, e * C:(e + 1) * C])
        whole_pass(w1[e], op1, 0, (P, 0))
        whole_pass(w1[e], op1, 1, (88, 56))
        last = keep.tile([P, PASS * J + 2 * PASS], BF16, name="last_block", align_bytes=64)
        first_sig = last[:, PASS * J - 32:PASS * J - 32 + 2 * PASS].bitcast(F32).rearrange("p (n t) -> p n t", t=J)
        sigs = [open_gates_into(first_sig, op1, e, 0)]
        raw_1 = load_columns(w3[e], 0, 0, PASS)
        raw_2 = load_columns(w3[e], 1, 0, PASS)
        raw_3 = load_columns(w3[e], 0, PASS, H)
        landing_b = raws.tile([P, J, PASS], F32, name="raw", align_bytes=512)
        raw_b = landing_b[:]
        for c0 in (0, PASS // 2):
            nc.sync.dma_start(out=raw_b[:, :, c0:c0 + PASS // 2],
                              in_=w3[e].rearrange("(g p j) c -> g p j c", p=P, j=J)[1][:, :, PASS + c0:PASS + c0 + PASS // 2])
        landing_c = raws.tile([P, B, J * N], F32, name="raw", align_bytes=512)
        raw_c, op_c = load_w2_halves(e - 1, landing_c), new_w2()
        landing_d = raws.tile([P, B, J * N], F32, name="raw", align_bytes=512)
        raw_d, op_d = load_w2_halves(e, landing_d), new_w2()
        late_gates = keep.tile([P, 2 * C], F32, name="late_gates", align_bytes=512)
        nc.sync.dma_start(late_gates[:], gate[:, 2 * C:])
        quantize_pass(block(raw_1, 0, 0, 64), op3, 0, 0, 1)
        quantize_pass(block(raw_2, 0, 0, 76), op3, 1, 0, 4)
        second_sig = raw_2.rearrange("p j c -> p (j c)")[:, :PASS].rearrange("p (n t) -> p n t", t=J)
        sigs.append(open_gates_into(second_sig, op1, e, 1))
        v0 = hidden_sums(op3, e, 0, "v")
        quantize_pass(block(raw_3, 0, 1, 64), op3, 0, 1, 1)
        h0 = product_into(raw_3.rearrange("p j c -> p (j c)")[:, :PASS // 2].bitcast(BF16), v0, sigs[0])
        quantize_hidden(h0, h_op, 0)
        grouped_b = last[:, :PASS * J]
        interleave(1, grouped_b, raw_b, 0, 0, 60)
        interleave(0, grouped_b, raw_b, 0, 60, 68)
        interleave(1, grouped_b, raw_b, 0, 68, 96)
        interleave(0, grouped_b, raw_b, 0, 96, P)
        for half in range(2):
            for t in range(J):
                first = t * P + half * (P // 2)
                cols = slice(PASS + first, PASS + first + P // 2)
                nc.vector.quantize_mx(out=op3[0][:, 1, cols].bitcast(FP8X4), scales=op3[1][:, 1, cols],
                                      in_=grouped_b[:, first * J:(first + P // 2) * J])
        v1 = grouped_sums(op3, e, 1)
        both_c = interleave_whole_w2(raw_c, 1)
        both_d = interleave_whole_w2(raw_d, 1)
        for b in range(B):
            quantize_w2(both_c[:, b], op_c, b)
        y_c = second_sums(op_c, h_ops[e - 1])
        h1 = product_into(raw_c.rearrange("p b j n -> p (b j n)")[:, PASS:PASS + PASS // 2].bitcast(BF16), v1, sigs[1])
        quantize_w2(both_d[:, 0], op_d, 0)
        gated_c = second_sig.rearrange("p n t -> p (n t)")[:, PASS - C:]
        nc.vector.tensor_tensor(gated_c, y_c[:], late_gates[:, :C], MULT)
        quantize_hidden(h1, h_op, 1)
        quantize_w2(both_d[:, 1], op_d, 1)
        y_d = second_sums(op_d, h_op)
        nc.scalar.activation(window[:].indirect(offsets[:, (e - 1) * (C // 16):e * (C // 16)]), gated_c, COPY)
        gated = new_y()
        nc.vector.tensor_tensor(gated, y_d[:], late_gates[:, C:], MULT)
        nc.vector.tensor_copy(window[:].indirect(offsets[:, e * (C // 16):]), gated)
        nc.sync.dma_start(out, window[:])
